import numpy as np
CORES = [14,30,46,62,78,94,110,126,6,22,38,54,70,86,102,118]
N = 16
ROOT = 11
def setup_inputs(rng):
    return {"x": rng.standard_normal((N, 128, 256), dtype=np.float32)}
def reference(x):
    return {"y": np.broadcast_to(x[ROOT], x.shape)}

@@ -1,0 +1,44 @@
+from concourse.bass import DstId, RemoteDMATransfer
+
+SCRATCH = {
+    "land": ("sbuf", [128, 256], "float32"),
+}
+SEMAPHORES = ["loaded", "arrived", "sent", "stored"]
+
+OFF_CHIP = 0x00FF
+NENG = 8
+
+
+def rank_program(g, core, T, topo):
+    rank = T.rank_of(core)
+    if rank is None:
+        return
+    root = T.cores[T.root]
+    my_chip = topo.chip(core)
+    mate = core ^ 8
+
+    if core == root:
+        g.sync.dma_start(T.land[:], T.x[:]).then_inc(T.sem.loaded, 16)
+        g.scalar.dma_start(T.y[:], T.x[:]).then_inc(T.sem.stored, 16)
+        dsts = [c for c in T.cores if c != root and (topo.same_plane(topo.chip(c), my_chip) or c == mate)]
+        ids = []
+        for c in dsts:
+            rid, pid, _se = topo.addr(c)
+            ids.append(DstId(rid=rid, pnc=pid))
+        g.wait_ge(T.sem.loaded, 16)
+        g.remote_dma_fused(
+            [RemoteDMATransfer(dst_ids=ids, dma_engine_mask=OFF_CHIP, remote_sem=T.sem.arrived,
+                               src=T.land[:], dsts=[T.land[:] for _c in dsts])],
+            local_sem=T.sem.sent)
+        g.wait_ge(T.sem.sent, NENG)
+        g.wait_ge(T.sem.stored, 16)
+        return
+
+    g.sync.wait_ge(T.sem.arrived, NENG)
+    g.sync.dma_start(T.y[:], T.land[:]).then_inc(T.sem.stored, 16)
+    g.wait_ge(T.sem.arrived, NENG)
+    if topo.same_plane(my_chip, topo.chip(root)):
+        rid, pid, _se = topo.addr(mate)
+        g.remote_dma(T.land[:], T.land[:], T.sem.arrived, T.sem.sent, pid, rid, OFF_CHIP)
+        g.wait_ge(T.sem.sent, NENG)
+    g.wait_ge(T.sem.stored, 16)

@@ -1,44 +1,102 @@
 from concourse.bass import DstId, RemoteDMATransfer
 
+NA, WA = 16, 9
+NB, WB = 14, 8
+ROWS_A = NA * WA * 128 // 256
+
 SCRATCH = {
-    "land": ("sbuf", [128, 256], "float32"),
+    "da": ("dram", [NA, 128, WA], "float32"),
+    "db": ("dram", [NB, 128, WB], "float32"),
 }
-SEMAPHORES = ["loaded", "arrived", "sent", "stored"]
+SEMAPHORES = ["lda", "ldb", "got", "arra", "arrb", "sent", "stored"]
 
 OFF_CHIP = 0x00FF
 NENG = 8
+HELPER = 2
+
+
+def make_plan(T, topo):
+    root = T.cores[T.root]
+    rc = topo.chip(root)
+    rank_k = root % 8
+    nine = [rc * 8 + HELPER, (rc ^ 1) * 8 + HELPER]
+    eight = []
+    i = 0
+    for pair in range(8):
+        if pair == rc // 2:
+            continue
+        for k in (rank_k, HELPER):
+            even = (2 * pair) * 8 + k
+            odd = (2 * pair + 1) * 8 + k
+            if i % 5 == 0:
+                nine.append(odd)
+                eight.append(even)
+            else:
+                nine.append(even)
+                eight.append(odd)
+            i += 1
+    return nine, eight
+
+
+def dst_id(topo, c):
+    rid, pid, _se = topo.addr(c)
+    return DstId(rid=rid, pnc=pid)
 
 
 def rank_program(g, core, T, topo):
-    rank = T.rank_of(core)
-    if rank is None:
-        return
     root = T.cores[T.root]
-    my_chip = topo.chip(core)
-    mate = core ^ 8
+    nine, eight = make_plan(T, topo)
+    sem = T.sem
 
     if core == root:
-        g.sync.dma_start(T.land[:], T.x[:]).then_inc(T.sem.loaded, 16)
-        g.scalar.dma_start(T.y[:], T.x[:]).then_inc(T.sem.stored, 16)
-        dsts = [c for c in T.cores if c != root and (topo.same_plane(topo.chip(c), my_chip) or c == mate)]
-        ids = []
-        for c in dsts:
-            rid, pid, _se = topo.addr(c)
-            ids.append(DstId(rid=rid, pnc=pid))
-        g.wait_ge(T.sem.loaded, 16)
-        g.remote_dma_fused(
-            [RemoteDMATransfer(dst_ids=ids, dma_engine_mask=OFF_CHIP, remote_sem=T.sem.arrived,
-                               src=T.land[:], dsts=[T.land[:] for _c in dsts])],
-            local_sem=T.sem.sent)
-        g.wait_ge(T.sem.sent, NENG)
-        g.wait_ge(T.sem.stored, 16)
+        g.sync.dma_start(T.da[:], T.x[0:ROWS_A, :]).then_inc(sem.lda, 16)
+        g.scalar.dma_start(T.db[:], T.x[ROWS_A:128, :]).then_inc(sem.ldb, 16)
+        n_sent = 0
+        for buf, agents, ld in ((T.da, nine, sem.lda), (T.db, eight, sem.ldb)):
+            g.wait_ge(ld, 16)
+            half = (len(agents) + 1) // 2
+            for lo, hi in ((0, half), (half, len(agents))):
+                g.remote_dma_fused(
+                    [RemoteDMATransfer(dst_ids=[dst_id(topo, agents[s])], dma_engine_mask=1 << (s - lo),
+                                       remote_sem=sem.got, src=buf[s], dst=buf[s])
+                     for s in range(lo, hi)],
+                    local_sem=sem.sent)
+                n_sent += hi - lo
+        g.sync.wait_ge(sem.sent, n_sent)
+        g.sync.dma_start(T.y[:], T.x[:]).then_inc(sem.stored, 16)
+        g.wait_ge(sem.sent, n_sent)
+        g.wait_ge(sem.stored, 16)
         return
 
-    g.sync.wait_ge(T.sem.arrived, NENG)
-    g.sync.dma_start(T.y[:], T.land[:]).then_inc(T.sem.stored, 16)
-    g.wait_ge(T.sem.arrived, NENG)
-    if topo.same_plane(my_chip, topo.chip(root)):
-        rid, pid, _se = topo.addr(mate)
-        g.remote_dma(T.land[:], T.land[:], T.sem.arrived, T.sem.sent, pid, rid, OFF_CHIP)
-        g.wait_ge(T.sem.sent, NENG)
-    g.wait_ge(T.sem.stored, 16)
+    is_rank = T.rank_of(core) is not None
+    in_a = core in nine
+    in_b = core in eight
+    if not (is_rank or in_a or in_b):
+        return
+
+    if in_a or in_b:
+        buf, slot, arr = (T.da, nine.index(core), sem.arra) if in_a else (T.db, eight.index(core), sem.arrb)
+        dsts = [c for c in T.cores if c != root and c != core]
+        g.wait_ge(sem.got, 1)
+        g.remote_dma_fused(
+            [RemoteDMATransfer(dst_ids=[dst_id(topo, c) for c in dsts], dma_engine_mask=OFF_CHIP,
+                               remote_sem=arr, src=buf[slot], dsts=[buf[slot] for _c in dsts])],
+            local_sem=sem.sent)
+
+    if is_rank:
+        need_a = NENG * (NA - (1 if in_a else 0))
+        need_b = NENG * (NB - (1 if in_b else 0))
+        if in_a:
+            g.sync.wait_ge(sem.got, 1)
+        g.sync.wait_ge(sem.arra, need_a)
+        g.sync.dma_start(T.y[0:ROWS_A, :], T.da[:]).then_inc(sem.stored, 16)
+        if in_b:
+            g.scalar.wait_ge(sem.got, 1)
+        g.scalar.wait_ge(sem.arrb, need_b)
+        g.scalar.dma_start(T.y[ROWS_A:128, :], T.db[:]).then_inc(sem.stored, 16)
+        g.wait_ge(sem.arra, need_a)
+        g.wait_ge(sem.arrb, need_b)
+        g.wait_ge(sem.stored, 32)
+
+    if in_a or in_b:
+        g.wait_ge(sem.sent, NENG)

from concourse.bass import DstId, RemoteDMATransfer

NA, WA = 16, 9
NB, WB = 14, 8
ROWS_A = NA * WA * 128 // 256

SCRATCH = {
    "da": ("dram", [NA, 128, WA], "float32"),
    "db": ("dram", [NB, 128, WB], "float32"),
}
SEMAPHORES = ["lda", "ldb", "got", "arra", "arrb", "sent", "stored"]

OFF_CHIP = 0x00FF
NENG = 8
HELPER = 2


def make_plan(T, topo):
    root = T.cores[T.root]
    rc = topo.chip(root)
    rank_k = root % 8
    nine = [rc * 8 + HELPER, (rc ^ 1) * 8 + HELPER]
    eight = []
    i = 0
    for pair in range(8):
        if pair == rc // 2:
            continue
        for k in (rank_k, HELPER):
            even = (2 * pair) * 8 + k
            odd = (2 * pair + 1) * 8 + k
            if i % 5 == 0:
                nine.append(odd)
                eight.append(even)
            else:
                nine.append(even)
                eight.append(odd)
            i += 1
    return nine, eight


def dst_id(topo, c):
    rid, pid, _se = topo.addr(c)
    return DstId(rid=rid, pnc=pid)


def rank_program(g, core, T, topo):
    root = T.cores[T.root]
    nine, eight = make_plan(T, topo)
    sem = T.sem

    if core == root:
        g.sync.dma_start(T.da[:], T.x[0:ROWS_A, :]).then_inc(sem.lda, 16)
        g.scalar.dma_start(T.db[:], T.x[ROWS_A:128, :]).then_inc(sem.ldb, 16)
        n_sent = 0
        for buf, agents, ld in ((T.da, nine, sem.lda), (T.db, eight, sem.ldb)):
            g.wait_ge(ld, 16)
            half = (len(agents) + 1) // 2
            for lo, hi in ((0, half), (half, len(agents))):
                g.remote_dma_fused(
                    [RemoteDMATransfer(dst_ids=[dst_id(topo, agents[s])], dma_engine_mask=1 << (s - lo),
                                       remote_sem=sem.got, src=buf[s], dst=buf[s])
                     for s in range(lo, hi)],
                    local_sem=sem.sent)
                n_sent += hi - lo
        g.sync.wait_ge(sem.sent, n_sent)
        g.sync.dma_start(T.y[:], T.x[:]).then_inc(sem.stored, 16)
        g.wait_ge(sem.sent, n_sent)
        g.wait_ge(sem.stored, 16)
        return

    is_rank = T.rank_of(core) is not None
    in_a = core in nine
    in_b = core in eight
    if not (is_rank or in_a or in_b):
        return

    if in_a or in_b:
        buf, slot, arr = (T.da, nine.index(core), sem.arra) if in_a else (T.db, eight.index(core), sem.arrb)
        dsts = [c for c in T.cores if c != root and c != core]
        g.wait_ge(sem.got, 1)
        g.remote_dma_fused(
            [RemoteDMATransfer(dst_ids=[dst_id(topo, c) for c in dsts], dma_engine_mask=OFF_CHIP,
                               remote_sem=arr, src=buf[slot], dsts=[buf[slot] for _c in dsts])],
            local_sem=sem.sent)

    if is_rank:
        need_a = NENG * (NA - (1 if in_a else 0))
        need_b = NENG * (NB - (1 if in_b else 0))
        if in_a:
            g.sync.wait_ge(sem.got, 1)
        g.sync.wait_ge(sem.arra, need_a)
        g.sync.dma_start(T.y[0:ROWS_A, :], T.da[:]).then_inc(sem.stored, 16)
        if in_b:
            g.scalar.wait_ge(sem.got, 1)
        g.scalar.wait_ge(sem.arrb, need_b)
        g.scalar.dma_start(T.y[ROWS_A:128, :], T.db[:]).then_inc(sem.stored, 16)
        g.wait_ge(sem.arra, need_a)
        g.wait_ge(sem.arrb, need_b)
        g.wait_ge(sem.stored, 32)

    if in_a or in_b:
        g.wait_ge(sem.sent, NENG)
